import numpy as np, ml_dtypes
CORES = [7,15,23,39,47,63,71,79,87,95,119,127]
N = 12
TK, NT = 128, 6
def setup_inputs(rng):
    x = rng.standard_normal((NT, 128, TK), dtype=np.float32).astype(ml_dtypes.bfloat16)
    return {"x": np.broadcast_to(x, (2, NT, 128, TK)).reshape(N, 128, TK).copy(), "w": rng.standard_normal((N, 128, NT * 128), dtype=np.float32).astype(ml_dtypes.bfloat16)}
def setup_inputs_big(rng):
    d = setup_inputs(rng)
    for k in ("x", "w"): d[k] = (d[k].astype(np.float32) * 1024.0).astype(d[k].dtype)
    return d
def setup_inputs_small(rng):
    d = setup_inputs(rng)
    for k in ("x", "w"): d[k] = (d[k].astype(np.float32) * (1 / 1024.0)).astype(d[k].dtype)
    return d
def setup_inputs_apart(rng):
    d = setup_inputs(rng)
    f = (10.0 ** rng.permutation(np.linspace(-1.5, 1.5, N))).astype(np.float32).reshape(N, 1, 1)
    for k in ("x", "w"): d[k] = (d[k].astype(np.float32) * f).astype(d[k].dtype)
    return d
def tie_inputs(x):
    x = dict(x)
    x["x"] = np.concatenate([x["x"][:NT], x["x"][:NT]])
    return x
def reference(x, w):
    X, W = x.astype(np.float64), w.astype(np.float64)
    y = np.stack([sum(W[r][:, 128 * j:128 * j + 128].T @ X[j if r < NT else j + NT] for j in range(NT)) for r in range(N)])
    return {"y": y.astype(ml_dtypes.bfloat16 if x.dtype != np.float64 else np.float64)}

from concourse.bass import DstId, RemoteDMATransfer

TK = 128
NT = 6
DRAM_SLOTS = 0

SCRATCH = {
    "land": ("dram", [NT, 128, TK], "bfloat16"),
    "xs": ("sbuf", [128, NT * TK], "bfloat16"),
    "ws": ("sbuf", [128, NT * 128], "bfloat16"),
    "ps": ("psum", [128, TK], "float32"),
    "ys": ("sbuf", [128, TK], "bfloat16"),
}
SEMAPHORES = (["ldx", "ldo", "ldw", "sent", "mm", "cp", "st"] + ["t%d" % j for j in range(NT)]
              + ["u%d" % j for j in range(NT)])

PLANS = {}


def way(topo, s, d):
    cs, cd, di = topo.chip(s), topo.chip(d), topo.die(s)
    if topo.mates(cs, cd):
        return [("mate", cs, di)]
    if topo.same_plane(cs, cd):
        return [("out", cs, di), ("in", cd, di)]
    m = [c for c in range(topo.CHIPS) if topo.mates(cs, c)][0]
    return [("mate", cs, di), ("out", m, di), ("in", cd, di)]


def make_plan(cores, topo):
    n = len(cores)
    nt = n // 2
    ways = {}
    for h in range(n):
        for r in range(n):
            if h != r and topo.may_write(cores[h], cores[r]):
                ways[(h, r)] = way(topo, cores[h], cores[r])
    pick = {}

    def cost():
        load = {}
        for sel in pick.values():
            for r, h in sel.items():
                for l in ways[(h, r)]:
                    load[l] = load.get(l, 0) + 1
        return (sum(load.values()), sum(v ** 3 for v in load.values()))

    before = None
    while before != pick:
        before = dict(pick)
        for j in range(nt):
            recv = [r for r in range(n) if r % nt != j]
            best = None
            for bits in range(1 << len(recv)):
                if bin(bits).count("1") * 2 != len(recv):
                    continue
                sel = {r: (j if (bits >> i) & 1 else j + nt) for i, r in enumerate(recv)}
                if any((h, r) not in ways for r, h in sel.items()):
                    continue
                pick[j] = sel
                c = cost()
                if best is None or c < best[0]:
                    best = (c, sel)
            pick[j] = best[1]

    edges = [(h, r) for j in range(nt) for r, h in pick[j].items()]
    slots = nt - 1
    groups = {}
    for e in edges:
        for k in [("from", e[0]), ("to", e[1])] + ways[e]:
            groups.setdefault(k, []).append(e)
    groups = {k: v for k, v in groups.items() if len(v) <= slots}
    of = {e: [k for k, v in groups.items() if e in v] for e in edges}
    used = {k: set() for k in groups}
    slot = {}

    def order(e):
        return list(range(slots)) if len(ways[e]) > 1 else list(range(slots - 1, -1, -1))

    def fill():
        if len(slot) == len(edges):
            return True
        best = None
        for e in edges:
            if e not in slot:
                free = [c for c in order(e) if all(c not in used[k] for k in of[e])]
                if best is None or len(free) < len(best[1]):
                    best = (e, free)
        e, free = best
        for c in free:
            slot[e] = c
            for k in of[e]:
                used[k].add(c)
            if fill():
                return True
            del slot[e]
            for k in of[e]:
                used[k].discard(c)
        return False

    assert fill()
    sends = {h: [r for s, r in sorted((slot[e], e[1]) for e in edges if e[0] == h)] for h in range(n)}
    takes = {r: [h for s, h in sorted((slot[e], e[0]) for e in edges if e[1] == r)] for r in range(n)}
    return sends, takes


def rank_program(g, core, T, topo):
    rank = T.rank_of(core)
    if rank is None:
        return
    cores = list(T.cores)
    key = tuple(cores)
    if key not in PLANS:
        PLANS[key] = make_plan(cores, topo)
    sends, takes = PLANS[key]
    own = rank % NT
    sem = T.sem

    def blk(j):
        return slice(j * TK, (j + 1) * TK)

    def mask_of(h):
        m = -1
        for r in sends[h]:
            m &= topo.mask(cores[h], cores[r])
        return m

    def engines_of(h):
        return bin(mask_of(h)).count("1")

    g.sync.dma_start(T.land[own], T.x[:, :]).then_inc(sem.ldx, 16)
    g.sync.dma_start(T.xs[:, blk(own)], T.x[:, :]).then_inc(sem.ldo, 16)
    g.sync.dma_start(T.ws[:, :], T.w[:, :]).then_inc(sem.ldw, 16)

    ids = []
    dsts = []
    for s, r in enumerate(sends[rank]):
        rid, pid, ring = topo.addr(cores[r])
        ids.append(DstId(rid=rid, pnc=pid))
        dsts.append(T.land[own] if s < DRAM_SLOTS else T.xs[:, blk(own)])
    g.wait_ge(sem.ldx, 16)
    g.remote_dma_fused(
        [RemoteDMATransfer(dst_ids=ids, dma_engine_mask=mask_of(rank), remote_sem=sem["t%d" % own],
                           srcs=[T.land[own]], dsts=dsts, alu_op=0)],
        local_sem=sem.sent)

    for s, h in enumerate(takes[rank]):
        if s < DRAM_SLOTS:
            j = h % NT
            q = g.scalar if s % 2 == 0 else g.sync
            q.wait_ge(sem["t%d" % j], engines_of(h))
            q.dma_start(T.xs[:, blk(j)], T.land[j]).then_inc(sem["u%d" % j], 16)

    g.tensor.wait_ge(sem.ldo, 16)
    g.tensor.wait_ge(sem.ldw, 16)
    g.tensor.matmul(T.ps[:, :], T.ws[:, own * 128:(own + 1) * 128], T.xs[:, blk(own)], True, False)
    order = [(s, h) for s, h in enumerate(takes[rank]) if s >= DRAM_SLOTS]
    order = order[:-1] + [(s, h) for s, h in enumerate(takes[rank]) if s < DRAM_SLOTS] + order[-1:]
    for i, (s, h) in enumerate(order):
        j = h % NT
        last = i == len(order) - 1
        if s < DRAM_SLOTS:
            g.tensor.wait_ge(sem["u%d" % j], 16)
        else:
            g.tensor.wait_ge(sem["t%d" % j], engines_of(h))
        mm = g.tensor.matmul(T.ps[:, :], T.ws[:, j * 128:(j + 1) * 128], T.xs[:, blk(j)], False, last)
        if last:
            mm.then_inc(sem.mm, 1)

    g.vector.wait_ge(sem.mm, 1)
    g.vector.tensor_copy(T.ys[:, :], T.ps[:, :]).then_inc(sem.cp, 1)
    g.sync.wait_ge(sem.cp, 1)
    g.sync.dma_start(T.y[:, :], T.ys[:, :]).then_inc(sem.st, 16)
    g.sync.wait_ge(sem.st, 16)
    g.wait_ge(sem.sent, engines_of(rank))
